import numpy as np
import ml_dtypes


def mxq(x, axis, fmt="e4m3"):
    dtype, down = {"e4m3": (ml_dtypes.float8_e4m3fn, 7), "e5m2": (ml_dtypes.float8_e5m2, 14)}[fmt]
    v = np.moveaxis(np.asarray(x, np.float32).astype(ml_dtypes.bfloat16).astype(np.float64), axis, -1)
    blocks = v.reshape(v.shape[:-1] + (-1, 32))
    amax = np.abs(blocks).max(-1, keepdims=True)
    byte = np.maximum(np.where(amax > 0, np.frexp(amax)[1] - 1 + 127, 0) - down, 1)
    scale = np.exp2(byte - 127.0)
    codes = (blocks / scale).astype(np.float32).astype(dtype).astype(np.float64)
    return np.moveaxis((codes * scale).reshape(v.shape), -1, axis)


WIDE = False


def mx_kscale(k):
    if not WIDE:
        return np.ones(k)
    levels = np.array([10, -10, 5, -5, 0])
    if k % 512:
        return np.exp2(np.random.permutation(np.resize(levels, k // 32))).repeat(32)
    a = np.empty((k // 512, 16))
    for p in range(k // 512):
        a[p, :8] = np.random.permutation(np.resize(levels, 8))
        for g in range(8):
            far = levels[np.abs(levels - a[p, g]) >= 10]
            a[p, g + 8] = far[np.random.randint(len(far))]
    return np.exp2(a.ravel()).repeat(32)


def f64(x):
    return np.asarray(x).astype(np.float64)


def striped(idx):
    return np.tile(np.asarray(idx).reshape(-1, 16).T, (8, 1)).astype(np.uint16)


def unstriped(offs):
    return offs[:16].T.reshape(-1).astype(np.int64)


def striped8(idx):
    return np.asarray(idx).reshape(8, -1, 16).transpose(0, 2, 1).reshape(128, -1).astype(np.uint16)


def unstriped8(offs):
    return offs.reshape(8, 16, -1).transpose(0, 2, 1).reshape(8, -1).astype(np.int64)


def pick8(x, idx, run):
    r = np.arange(len(x))
    return x[r[:, None], idx[r % (8 * run) // run]]


E2M1 = np.array([0.0, 0.5, 1.0, 1.5, 2.0, 3.0, 4.0, 6.0, -0.0, -0.5, -1.0, -1.5, -2.0, -3.0, -4.0, -6.0])


def pack_weight(w, fmt):
    k, n = w.shape
    w = f64(np.asarray(w, np.float32).astype(ml_dtypes.bfloat16)).reshape(k // 32, 32, n)
    amax = np.abs(w).max(1)
    if fmt == "e4m3":
        byte = np.frexp(amax)[1] - 1 + 127 - 7
    else:
        mant, ex = np.frexp(amax / 6.0)
        byte = np.where(mant > 0.5, ex, ex - 1) + 127
    byte = np.clip(np.where(amax > 0, byte, 1), 1, 254)
    scaled = (w * np.exp2(127.0 - byte)[:, None, :]).reshape(k, n).astype(np.float32)
    by_word = np.ascontiguousarray(scaled.reshape(k // 512, 128, 4, n).transpose(0, 1, 3, 2))
    if fmt == "e4m3":
        words = by_word.astype(ml_dtypes.float8_e4m3fn).view(np.uint8)
    else:
        c = by_word.astype(ml_dtypes.float4_e2m1fn).view(np.uint8) & 0xF
        words = (c[..., 0::2] | (c[..., 1::2] << 4)).reshape(k // 512, 128, 2 * n)
    return np.ascontiguousarray(words), np.ascontiguousarray(byte.astype(np.uint8).reshape(k // 512, 16, n))


def unpack_weight(words, scales, fmt):
    g, _, n = scales.shape
    words = np.ascontiguousarray(words).reshape(g, 128, n, -1)
    if fmt == "e4m3":
        vals = words.view(ml_dtypes.float8_e4m3fn).astype(np.float64)
    else:
        nib = np.empty((g, 128, n, 4), np.uint8)
        nib[..., 0::2] = words & 0xF
        nib[..., 1::2] = words >> 4
        vals = E2M1[nib]
    vals = vals * np.repeat(np.exp2(scales.astype(np.float64) - 127.0), 8, axis=1)[..., None]
    return vals.transpose(0, 1, 3, 2).reshape(g * 512, n)


K, R, F, T, J, U = 512, 128, 512, 2048, 512, 1024


def setup_inputs():
    n = np.random.standard_normal
    idx = np.random.permutation(T)[:J]
    idx2 = np.stack([np.random.permutation(U)[:J] for _ in range(8)])
    idx3 = np.stack([np.random.permutation(U)[:J] for _ in range(8)])
    fk = mx_kscale(K)
    dtabp = pack_weight(n((K, T)) / fk[:, None], "e4m3")
    tabp = pack_weight(n((K, T)) / fk[:, None], "e4m3")
    return {
        "dtab_words": dtabp[0],
        "dtab_scales": dtabp[1],
        "tab_words": tabp[0],
        "tab_scales": tabp[1],
        "w1": (n((K, R)) * 1 / np.sqrt(K) * fk[:, None]).astype(np.float32),
        "gain": (np.random.uniform(0.5, 1.5, (R, 1))).astype(np.float32),
        "ground": (n((R, U)) * 0.7).astype(np.float32),
        "og": (np.random.uniform(0.5, 2.0, (R, 1))).astype(np.float32),
        "base": (0.3 * n((R, U))).astype(np.float32),
        "offs": striped(idx),
        "offs2": striped8(idx2),
        "offs3": striped8(idx3),
    }


def reference(dtab_words, dtab_scales, tab_words, tab_scales, w1, gain, ground, og, base, offs, offs2, offs3):
    idx = unstriped(offs)
    idx2 = unstriped8(offs2)
    idx3 = unstriped8(offs3)
    dtabu = unpack_weight(dtab_words, dtab_scales, "e4m3")
    tabu = unpack_weight(tab_words, tab_scales, "e4m3")
    w1q = mxq(f64(w1), 0, "e4m3")
    tabidxg = tabu[:, idx]
    a = w1q.T @ tabidxg
    dtabidxg = dtabu[:, idx]
    ta = w1q.T @ dtabidxg
    h0 = np.tanh(a)
    h1 = h0 * f64(gain)
    pa = np.zeros((R, U))
    pa[np.arange(R)[:, None], idx2[np.arange(R) % 128 // 16]] = h1
    pb = np.zeros((R, U))
    pb[np.arange(R)[:, None], idx3[np.arange(R) % 128 // 16]] = a
    xh0 = ta * (1.0 - np.square(h0))
    xh1 = xh0 * f64(gain)
    xpa = np.zeros((R, U))
    xpa[np.arange(R)[:, None], idx2[np.arange(R) % 128 // 16]] = xh1
    xpb = np.zeros((R, U))
    xpb[np.arange(R)[:, None], idx3[np.arange(R) % 128 // 16]] = ta
    xu1 = (xpa - xpb * pb * 2.0 * (pa + f64(ground)) / (np.square(pb) + 1.0)) / (np.square(pb) + 1.0)
    y = xu1 * f64(og) + f64(base)
    return y

@@ -1,0 +1,162 @@
+from contextlib import ExitStack
+
+import concourse.mybir as mybir
+from concourse.masks import make_identity
+
+F32 = mybir.dt.float32
+BF16 = mybir.dt.bfloat16
+U32 = mybir.dt.uint32
+I32 = mybir.dt.int32
+U16 = mybir.dt.uint16
+U8 = mybir.dt.uint8
+FP8X4 = mybir.dt.float8_e4m3fn_x4
+ACT = mybir.ActivationFunctionType
+ALU = mybir.AluOpType
+
+P = 128
+K, R, T, J, U = 512, 128, 2048, 512, 1024
+BANK = 512
+FLOPS = 2 * 2 * K * R * J
+
+
+def tile_attend_tcpageratio_kernel(tc, dtab_words, dtab_scales, tab_words, tab_scales, w1, gain, ground, og, base, offs, offs2, offs3, out):
+    nc = tc.nc
+    with ExitStack() as ctx:
+        sb = ctx.enter_context(tc.tile_pool(name="sb", bufs=1))
+        ps = ctx.enter_context(tc.psum_pool(name="ps", bufs=1))
+
+        def tile(name, shape, dtype, tag=None):
+            return sb.tile(shape, dtype, name=name, tag=tag or name, align_bytes=64)
+
+        offs_sb = tile("offs_sb", [P, J // 16], U16)
+        offs2_sb = tile("offs2_sb", [P, J // 16], U16)
+        offs3_sb = tile("offs3_sb", [P, J // 16], U16)
+        w_raw = tile("w_raw", [P, 4, R], F32)
+        tab_w = tile("tab_w", [P, T], I32)
+        dtab_w = tile("dtab_w", [P, T], I32)
+        tab_s = tile("tab_s", [P, T], U8)
+        dtab_s = tile("dtab_s", [P, T], U8)
+        gain_sb = tile("gain_sb", [P, 1], F32)
+        og_sb = tile("og_sb", [P, 1], F32)
+
+        nc.vector.memset(tab_s[:].bitcast(I32), 0)
+        nc.gpsimd.memset(dtab_s[:].bitcast(I32), 0)
+        nc.sync.dma_start(offs_sb[:], offs)
+        nc.scalar.dma_start(w_raw[:], w1.rearrange("(p t) r -> p t r", t=4))
+        for i in range(4):
+            nc.scalar.dma_start(tab_s[i:P:32, :].bitcast(I32), tab_scales[0, i:16:4, :].bitcast(I32))
+        for i in range(4):
+            nc.gpsimd.dma_start(dtab_s[i:P:32, :].bitcast(I32), dtab_scales[0, i:16:4, :].bitcast(I32))
+        nc.sync.dma_start(tab_w[:], tab_words[0].rearrange("p c t -> p (c t)").bitcast(I32))
+        nc.sync.dma_start(dtab_w[:], dtab_words[0].rearrange("p c t -> p (c t)").bitcast(I32))
+        nc.sync.dma_start(offs2_sb[:], offs2)
+        nc.sync.dma_start(offs3_sb[:], offs3)
+        nc.gpsimd.dma_start(gain_sb[:], gain)
+        nc.gpsimd.dma_start(og_sb[:], og)
+
+        pa = tile("pa", [P, U], F32)
+        dpage = tile("dpage", [P, U], F32)
+        xpage = tile("xpage", [P, U], F32)
+        cpage = tile("cpage", [P, U], F32)
+        ident = tile("ident", [P, P], F32)
+        nc.vector.memset(pa[:], 0.0)
+        nc.vector.memset(dpage[:], 1.0)
+        make_identity(nc, ident[:])
+        nc.gpsimd.memset(xpage[:], 0.0)
+        nc.gpsimd.memset(cpage[:], 0.0)
+
+        w_bf = tile("w_bf", [P, R, 4], BF16)
+        w_codes = tile("w_codes", [P, R], U32)
+        w_scales = tile("w_scales", [P, R], U8)
+        nc.scalar.activation(w_bf[:], w_raw[:].rearrange("p t r -> p r t"), ACT.Copy)
+        nc.vector.quantize_mx(out=w_codes[:].bitcast(FP8X4), scales=w_scales[:], in_=w_bf[:].rearrange("p r t -> p (r t)"))
+
+        def product(name, words, scales, tag):
+            g_s = tile(name + "_gs", [P, J], U8, tag)
+            g_w = tile(name + "_gw", [P, J], U32)
+            nc.vector.tensor_copy(g_s[:], scales[:].indirect(offs_sb[:]))
+            nc.vector.tensor_copy(g_w[:], words[:].bitcast(U32).indirect(offs_sb[:]))
+            acc = ps.tile([P, J], F32, name=name + "_acc")
+            nc.tensor.matmul_mx(out=acc[:], lhsT=w_codes[:].bitcast(FP8X4), lhsT_scale=w_scales[:],
+                                rhs=g_w[:].bitcast(FP8X4), rhs_scale=g_s[:], start=True, stop=True)
+            return acc
+
+        a = product("tab", tab_w, tab_s, None)
+        ta = product("dtab", dtab_w, dtab_s, "tab_w")
+        ground_sb = tile("ground_sb", [P, U], F32, "tab_s")
+        base_sb = tile("base_sb", [P, U], F32, "w_raw")
+        nc.sync.dma_start(ground_sb[:], ground)
+        nc.sync.dma_start(base_sb[:], base)
+
+        h0 = tile("h0", [P, J], F32)
+        h1 = tile("h1", [P, J], F32)
+        a_sq = tile("a_sq", [P, J], F32)
+        root = tile("root", [P, J], F32)
+        d1 = tile("d1", [P, J], F32)
+        d2 = tile("d2", [P, J], F32)
+        h_sq = tile("h_sq", [P, J], F32)
+        slope = tile("slope", [P, J], F32)
+        ta_og = tile("ta_og", [P, J], F32)
+        curve = tile("curve", [P, J], F32)
+        neg_gain = tile("neg_gain", [P, 1], F32)
+
+        nc.scalar.activation(neg_gain[:], gain_sb[:], ACT.Copy, scale=-1.0)
+        nc.scalar.activation(h0[:], a[:], ACT.Tanh)
+        nc.scalar.activation(h1[:], h0[:], ACT.Copy, scale=gain_sb[:])
+        nc.vector.tensor_copy(pa[:].indirect(offs2_sb[:]), h1[:])
+
+        nc.scalar.activation(a_sq[:], a[:], ACT.Square)
+        nc.scalar.activation(root[:], a_sq[:], ACT.Abs_reciprocal_sqrt, bias=1.0)
+        nc.scalar.activation(d1[:], root[:], ACT.Square)
+        nc.vector.tensor_copy(dpage[:].indirect(offs3_sb[:]), d1[:])
+
+        nc.scalar.activation(h_sq[:], h0[:], ACT.Square)
+        nc.scalar.activation(slope[:], h_sq[:], ACT.Identity, scale=neg_gain[:], bias=gain_sb[:])
+        nc.scalar.activation(ta_og[:], ta[:], ACT.Copy, scale=og_sb[:])
+        nc.vector.tensor_tensor(xpage[:].indirect(offs2_sb[:]), ta_og[:], slope[:], ALU.mult)
+
+        nc.scalar.activation(d2[:], d1[:], ACT.Square)
+        nc.vector.scalar_tensor_tensor(curve[:], a[:], -2.0, d2[:], ALU.mult, ALU.mult)
+
+        def add_in_psum(name, x, y):
+            banks = []
+            for half in range(U // BANK):
+                turned = ps.tile([P, BANK], F32, name=name + "_turned", tag="turned%d" % half)
+                for b in range(BANK // P):
+                    src = slice(half * BANK + b * P, half * BANK + (b + 1) * P)
+                    dst = slice(b * P, (b + 1) * P)
+                    nc.tensor.matmul(turned[:, dst], lhsT=y[:, src], rhs=ident[:], is_transpose=True, start=True, stop=False)
+                    nc.tensor.matmul(turned[:, dst], lhsT=x[:, src], rhs=ident[:], is_transpose=True, start=False, stop=True)
+                turned_sb = tile("%s_turned_sb%d" % (name, half), [P, BANK], F32)
+                nc.scalar.copy(turned_sb[:], turned[:])
+                total = ps.tile([P, BANK], F32, name="%s_sum%d" % (name, half))
+                for b in range(BANK // P):
+                    dst = slice(b * P, (b + 1) * P)
+                    nc.tensor.transpose(total[:, dst], turned_sb[:, dst], ident[:])
+                banks.append(total)
+            return banks
+
+        t1 = add_in_psum("t1", pa, ground_sb)
+        upage = tile("upage", [P, U], F32)
+        for half in range(U // BANK):
+            cols = slice(half * BANK, (half + 1) * BANK)
+            nc.vector.tensor_tensor(upage[:, cols], xpage[:, cols], dpage[:, cols], ALU.mult)
+        v = add_in_psum("v", upage, base_sb)
+        nc.vector.tensor_tensor(cpage[:].indirect(offs3_sb[:]), ta_og[:], curve[:], ALU.mult)
+
+        CH = 256
+        n = U // CH
+        prods = [tile("prod%d" % c, [P, CH], F32) for c in range(n)]
+        outs = [tile("res%d" % c, [P, CH], F32) for c in range(n)]
+
+        def bank_cols(c):
+            return c * CH // BANK, slice(c * CH % BANK, c * CH % BANK + CH)
+
+        for c in range(n + 1):
+            if c < n:
+                half, cols = bank_cols(c)
+                nc.vector.tensor_tensor(prods[c][:], cpage[:, c * CH:(c + 1) * CH], t1[half][:, cols], ALU.mult)
+            if c > 0:
+                half, cols = bank_cols(c - 1)
+                nc.vector.tensor_tensor(outs[c - 1][:], prods[c - 1][:], v[half][:, cols], ALU.add)
+                nc.sync.dma_start(out[:, (c - 1) * CH:c * CH], outs[c - 1][:])

@@ -33,63 +33,61 @@ def tile_attend_tcpageratio_kernel(tc, dtab_words, dtab_scales, tab_words, tab_s
         offs3_sb = tile("offs3_sb", [P, J // 16], U16)
         w_raw = tile("w_raw", [P, 4, R], F32)
         tab_w = tile("tab_w", [P, T], I32)
-        dtab_w = tile("dtab_w", [P, T], I32)
         tab_s = tile("tab_s", [P, T], U8)
         dtab_s = tile("dtab_s", [P, T], U8)
-        gain_sb = tile("gain_sb", [P, 1], F32)
-        og_sb = tile("og_sb", [P, 1], F32)
 
-        nc.vector.memset(tab_s[:].bitcast(I32), 0)
+        nc.gpsimd.memset(tab_s[:].bitcast(I32), 0)
         nc.gpsimd.memset(dtab_s[:].bitcast(I32), 0)
         nc.sync.dma_start(offs_sb[:], offs)
-        nc.scalar.dma_start(w_raw[:], w1.rearrange("(p t) r -> p t r", t=4))
-        for i in range(4):
-            nc.scalar.dma_start(tab_s[i:P:32, :].bitcast(I32), tab_scales[0, i:16:4, :].bitcast(I32))
-        for i in range(4):
-            nc.gpsimd.dma_start(dtab_s[i:P:32, :].bitcast(I32), dtab_scales[0, i:16:4, :].bitcast(I32))
-        nc.sync.dma_start(tab_w[:], tab_words[0].rearrange("p c t -> p (c t)").bitcast(I32))
-        nc.sync.dma_start(dtab_w[:], dtab_words[0].rearrange("p c t -> p (c t)").bitcast(I32))
         nc.sync.dma_start(offs2_sb[:], offs2)
+        nc.sync.dma_start(w_raw[:], w1.rearrange("(p t) r -> p t r", t=4))
+        for i in range(4):
+            nc.sync.dma_start(tab_s[i:P:32, :].bitcast(I32), tab_scales[0, i:16:4, :].bitcast(I32))
+        nc.sync.dma_start(tab_w[:], tab_words[0].rearrange("p c t -> p (c t)").bitcast(I32))
         nc.sync.dma_start(offs3_sb[:], offs3)
-        nc.gpsimd.dma_start(gain_sb[:], gain)
-        nc.gpsimd.dma_start(og_sb[:], og)
-
-        pa = tile("pa", [P, U], F32)
-        dpage = tile("dpage", [P, U], F32)
-        xpage = tile("xpage", [P, U], F32)
-        cpage = tile("cpage", [P, U], F32)
-        ident = tile("ident", [P, P], F32)
-        nc.vector.memset(pa[:], 0.0)
-        nc.vector.memset(dpage[:], 1.0)
-        make_identity(nc, ident[:])
-        nc.gpsimd.memset(xpage[:], 0.0)
-        nc.gpsimd.memset(cpage[:], 0.0)
 
         w_bf = tile("w_bf", [P, R, 4], BF16)
         w_codes = tile("w_codes", [P, R], U32)
         w_scales = tile("w_scales", [P, R], U8)
-        nc.scalar.activation(w_bf[:], w_raw[:].rearrange("p t r -> p r t"), ACT.Copy)
+        nc.vector.tensor_copy(w_bf[:], w_raw[:].rearrange("p t r -> p r t"))
         nc.vector.quantize_mx(out=w_codes[:].bitcast(FP8X4), scales=w_scales[:], in_=w_bf[:].rearrange("p r t -> p (r t)"))
 
-        def product(name, words, scales, tag):
-            g_s = tile(name + "_gs", [P, J], U8, tag)
-            g_w = tile(name + "_gw", [P, J], U32)
-            nc.vector.tensor_copy(g_s[:], scales[:].indirect(offs_sb[:]))
-            nc.vector.tensor_copy(g_w[:], words[:].bitcast(U32).indirect(offs_sb[:]))
-            acc = ps.tile([P, J], F32, name=name + "_acc")
-            nc.tensor.matmul_mx(out=acc[:], lhsT=w_codes[:].bitcast(FP8X4), lhsT_scale=w_scales[:],
-                                rhs=g_w[:].bitcast(FP8X4), rhs_scale=g_s[:], start=True, stop=True)
-            return acc
+        pa = tile("pa", [P, U], F32)
+        dpage = tile("dpage", [P, U], F32)
+        xpage = tile("xpage", [P, U], F32)
+        ident = tile("ident", [P, P], F32)
+        nc.vector.memset(pa[:], 0.0)
+        nc.vector.memset(dpage[:], 1.0)
+        make_identity(nc, ident[:])
+        nc.vector.memset(xpage[:], 0.0)
+        for i in range(4):
+            nc.sync.dma_start(dtab_s[i:P:32, :].bitcast(I32), dtab_scales[0, i:16:4, :].bitcast(I32))
 
-        a = product("tab", tab_w, tab_s, None)
-        ta = product("dtab", dtab_w, dtab_s, "tab_w")
-        ground_sb = tile("ground_sb", [P, U], F32, "tab_s")
-        base_sb = tile("base_sb", [P, U], F32, "w_raw")
-        nc.sync.dma_start(ground_sb[:], ground)
-        nc.sync.dma_start(base_sb[:], base)
 
-        h0 = tile("h0", [P, J], F32)
-        h1 = tile("h1", [P, J], F32)
+        dtab_w = tile("dtab_w", [P, T], I32, "w_raw")
+        nc.sync.dma_start(dtab_w[:], dtab_words[0].rearrange("p c t -> p (c t)").bitcast(I32))
+
+        HALF = J // 2
+        tab_gs = tile("tab_gs", [P, J], U8)
+        tab_gw = tile("tab_gw", [P, J], U32)
+        nc.vector.tensor_copy(tab_gs[:], tab_s[:].indirect(offs_sb[:]))
+        a = []
+        h0 = []
+        for s in range(2):
+            slots = slice(s * HALF, (s + 1) * HALF)
+            entries = slice(s * HALF // 16, (s + 1) * HALF // 16)
+            nc.vector.tensor_copy(tab_gw[:, slots], tab_w[:].bitcast(U32).indirect(offs_sb[:, entries]))
+            a.append(ps.tile([P, HALF], F32, name="a%d" % s))
+            nc.tensor.matmul_mx(out=a[s][:], lhsT=w_codes[:].bitcast(FP8X4), lhsT_scale=w_scales[:],
+                                rhs=tab_gw[:, slots].bitcast(FP8X4), rhs_scale=tab_gs[:, slots], start=True, stop=True)
+            h0.append(tile("h0_%d" % s, [P, HALF], F32))
+            nc.scalar.activation(h0[s][:], a[s][:], ACT.Tanh)
+        cpage = tile("cpage", [P, U], F32, "tab_w")
+        nc.vector.memset(cpage[:], 0.0)
+        for s in range(2):
+            entries = slice(s * HALF // 16, (s + 1) * HALF // 16)
+            nc.vector.tensor_copy(pa[:].indirect(offs2_sb[:, entries]), h0[s][:])
+
         a_sq = tile("a_sq", [P, J], F32)
         root = tile("root", [P, J], F32)
         d1 = tile("d1", [P, J], F32)
@@ -97,66 +95,89 @@ def tile_attend_tcpageratio_kernel(tc, dtab_words, dtab_scales, tab_words, tab_s
         h_sq = tile("h_sq", [P, J], F32)
         slope = tile("slope", [P, J], F32)
         ta_og = tile("ta_og", [P, J], F32)
-        curve = tile("curve", [P, J], F32)
         neg_gain = tile("neg_gain", [P, 1], F32)
+        for s in range(2):
+            slots = slice(s * HALF, (s + 1) * HALF)
+            nc.scalar.activation(a_sq[:, slots], a[s][:], ACT.Square)
+            nc.scalar.activation(h_sq[:, slots], h0[s][:], ACT.Square)
 
-        nc.scalar.activation(neg_gain[:], gain_sb[:], ACT.Copy, scale=-1.0)
-        nc.scalar.activation(h0[:], a[:], ACT.Tanh)
-        nc.scalar.activation(h1[:], h0[:], ACT.Copy, scale=gain_sb[:])
-        nc.vector.tensor_copy(pa[:].indirect(offs2_sb[:]), h1[:])
+        a2 = tile("a2", [P, J], F32)
+        curve = tile("curve", [P, J], F32)
+        cvals = tile("cvals", [P, J], F32)
+        xvals = tile("xvals", [P, J], F32)
+        for s in range(2):
+            slots = slice(s * HALF, (s + 1) * HALF)
+            nc.scalar.activation(a2[:, slots], a[s][:], ACT.Copy, scale=-2.0)
 
-        nc.scalar.activation(a_sq[:], a[:], ACT.Square)
+        gain_sb = tile("gain_sb", [P, 1], F32, "tab_s")
+        og_sb = tile("og_sb", [P, 1], F32, "w_bf")
+        nc.sync.dma_start(gain_sb[:], gain)
+        nc.sync.dma_start(og_sb[:], og)
+
+        dtab_gs = tile("dtab_gs", [P, J], U8, "h0_0")
+        dtab_gw = tile("dtab_gw", [P, J], U32, "h0_1")
+        nc.vector.tensor_copy(dtab_gs[:], dtab_s[:].indirect(offs_sb[:]))
+        nc.vector.tensor_copy(dtab_gw[:], dtab_w[:].bitcast(U32).indirect(offs_sb[:]))
+        ta = ps.tile([P, J], F32, name="ta")
+        nc.tensor.matmul_mx(out=ta[:], lhsT=w_codes[:].bitcast(FP8X4), lhsT_scale=w_scales[:],
+                            rhs=dtab_gw[:].bitcast(FP8X4), rhs_scale=dtab_gs[:], start=True, stop=True)
+        ground_sb = tile("ground_sb", [P, U], F32, "tab_gw")
+        base_sb = tile("base_sb", [P, U], F32, "tab_gs")
+        nc.sync.dma_start(ground_sb[:], ground)
+        nc.sync.dma_start(base_sb[:], base)
+
         nc.scalar.activation(root[:], a_sq[:], ACT.Abs_reciprocal_sqrt, bias=1.0)
         nc.scalar.activation(d1[:], root[:], ACT.Square)
         nc.vector.tensor_copy(dpage[:].indirect(offs3_sb[:]), d1[:])
 
-        nc.scalar.activation(h_sq[:], h0[:], ACT.Square)
+        nc.scalar.activation(d2[:], d1[:], ACT.Square)
+        nc.gpsimd.tensor_tensor(curve[:], a2[:], d2[:], ALU.mult)
+        nc.scalar.activation(neg_gain[:], gain_sb[:], ACT.Copy, scale=-1.0)
         nc.scalar.activation(slope[:], h_sq[:], ACT.Identity, scale=neg_gain[:], bias=gain_sb[:])
         nc.scalar.activation(ta_og[:], ta[:], ACT.Copy, scale=og_sb[:])
-        nc.vector.tensor_tensor(xpage[:].indirect(offs2_sb[:]), ta_og[:], slope[:], ALU.mult)
+        nc.gpsimd.tensor_tensor(xvals[:], ta_og[:], slope[:], ALU.mult)
+        nc.vector.tensor_copy(xpage[:].indirect(offs2_sb[:]), xvals[:])
 
-        nc.scalar.activation(d2[:], d1[:], ACT.Square)
-        nc.vector.scalar_tensor_tensor(curve[:], a[:], -2.0, d2[:], ALU.mult, ALU.mult)
 
-        def add_in_psum(name, x, y):
-            banks = []
-            for half in range(U // BANK):
-                turned = ps.tile([P, BANK], F32, name=name + "_turned", tag="turned%d" % half)
-                for b in range(BANK // P):
-                    src = slice(half * BANK + b * P, half * BANK + (b + 1) * P)
-                    dst = slice(b * P, (b + 1) * P)
-                    nc.tensor.matmul(turned[:, dst], lhsT=y[:, src], rhs=ident[:], is_transpose=True, start=True, stop=False)
-                    nc.tensor.matmul(turned[:, dst], lhsT=x[:, src], rhs=ident[:], is_transpose=True, start=False, stop=True)
-                turned_sb = tile("%s_turned_sb%d" % (name, half), [P, BANK], F32)
-                nc.scalar.copy(turned_sb[:], turned[:])
-                total = ps.tile([P, BANK], F32, name="%s_sum%d" % (name, half))
-                for b in range(BANK // P):
-                    dst = slice(b * P, (b + 1) * P)
-                    nc.tensor.transpose(total[:, dst], turned_sb[:, dst], ident[:])
-                banks.append(total)
-            return banks
+        nc.gpsimd.tensor_tensor(cvals[:], curve[:], ta_og[:], ALU.mult)
+        nc.vector.tensor_copy(cpage[:].indirect(offs3_sb[:]), cvals[:])
 
-        t1 = add_in_psum("t1", pa, ground_sb)
+        def add_in_psum(name, x, y, tag, turned_tag):
+            turned = ps.tile([P, BANK], F32, name=name + "_turned", tag=turned_tag)
+            for b in range(BANK // P):
+                blk = slice(b * P, (b + 1) * P)
+                nc.tensor.matmul(turned[:, blk], lhsT=y[:, blk], rhs=ident[:], is_transpose=True, start=True, stop=False)
+                nc.tensor.matmul(turned[:, blk], lhsT=x[:, blk], rhs=ident[:], is_transpose=True, start=False, stop=True)
+            turned_sb = tile(name + "_turned_sb", [P, BANK], F32)
+            nc.scalar.copy(turned_sb[:], turned[:])
+            total = ps.tile([P, BANK], F32, name=name, tag=tag)
+            for b in range(BANK // P):
+                blk = slice(b * P, (b + 1) * P)
+                nc.tensor.transpose(total[:, blk], turned_sb[:, blk], ident[:])
+            return total
+
+        pa_g = tile("pa_g", [P, U], F32)
+        t1 = []
+        for half in range(U // BANK):
+            cols = slice(half * BANK, (half + 1) * BANK)
+            nc.scalar.activation(pa_g[:, cols], pa[:, cols], ACT.Copy, scale=gain_sb[:])
+            t1.append(add_in_psum("t1_%d" % half, pa_g[:, cols], ground_sb[:, cols], "t1_%d" % half, "turned%d" % half))
         upage = tile("upage", [P, U], F32)
         for half in range(U // BANK):
             cols = slice(half * BANK, (half + 1) * BANK)
-            nc.vector.tensor_tensor(upage[:, cols], xpage[:, cols], dpage[:, cols], ALU.mult)
-        v = add_in_psum("v", upage, base_sb)
-        nc.vector.tensor_tensor(cpage[:].indirect(offs3_sb[:]), ta_og[:], curve[:], ALU.mult)
+            nc.gpsimd.tensor_tensor(upage[:, cols], xpage[:, cols], dpage[:, cols], ALU.mult)
+        v1 = tile("v1", [P, BANK], F32)
+        nc.gpsimd.tensor_tensor(v1[:], upage[:, BANK:U], base_sb[:, BANK:U], ALU.add)
+        v = [add_in_psum("v0", upage[:, 0:BANK], base_sb[:, 0:BANK], "v0", "turned0"), v1]
 
-        CH = 256
-        n = U // CH
-        prods = [tile("prod%d" % c, [P, CH], F32) for c in range(n)]
-        outs = [tile("res%d" % c, [P, CH], F32) for c in range(n)]
-
-        def bank_cols(c):
-            return c * CH // BANK, slice(c * CH % BANK, c * CH % BANK + CH)
-
-        for c in range(n + 1):
-            if c < n:
-                half, cols = bank_cols(c)
-                nc.vector.tensor_tensor(prods[c][:], cpage[:, c * CH:(c + 1) * CH], t1[half][:, cols], ALU.mult)
-            if c > 0:
-                half, cols = bank_cols(c - 1)
-                nc.vector.tensor_tensor(outs[c - 1][:], prods[c - 1][:], v[half][:, cols], ALU.add)
-                nc.sync.dma_start(out[:, (c - 1) * CH:c * CH], outs[c - 1][:])
+        prods = {}
+        for half in (1, 0):
+            cols = slice(half * BANK, (half + 1) * BANK)
+            prods[half] = tile("prod%d" % half, [P, BANK], F32)
+            nc.vector.tensor_tensor(prods[half][:], cpage[:, cols], t1[half][:], ALU.mult)
+        for lo, hi in ((512, 1024), (0, 256), (256, 512)):
+            half, first = divmod(lo, BANK)
+            cols = slice(first, first + hi - lo)
+            res = tile("res%d" % lo, [P, hi - lo], F32)
+            nc.vector.tensor_tensor(res[:], prods[half][:, cols], v[half][:, cols], ALU.add)
+            nc.sync.dma_start(out[:, lo:hi], res[:])

@@ -44,7 +44,6 @@ def tile_attend_tcpageratio_kernel(tc, dtab_words, dtab_scales, tab_words, tab_s
         for i in range(4):
             nc.sync.dma_start(tab_s[i:P:32, :].bitcast(I32), tab_scales[0, i:16:4, :].bitcast(I32))
         nc.sync.dma_start(tab_w[:], tab_words[0].rearrange("p c t -> p (c t)").bitcast(I32))
-        nc.sync.dma_start(offs3_sb[:], offs3)
 
         w_bf = tile("w_bf", [P, R, 4], BF16)
         w_codes = tile("w_codes", [P, R], U32)
@@ -54,14 +53,13 @@ def tile_attend_tcpageratio_kernel(tc, dtab_words, dtab_scales, tab_words, tab_s
 
         pa = tile("pa", [P, U], F32)
         dpage = tile("dpage", [P, U], F32)
-        xpage = tile("xpage", [P, U], F32)
         ident = tile("ident", [P, P], F32)
         nc.vector.memset(pa[:], 0.0)
         nc.vector.memset(dpage[:], 1.0)
         make_identity(nc, ident[:])
-        nc.vector.memset(xpage[:], 0.0)
         for i in range(4):
             nc.sync.dma_start(dtab_s[i:P:32, :].bitcast(I32), dtab_scales[0, i:16:4, :].bitcast(I32))
+        nc.sync.dma_start(offs3_sb[:], offs3)
 
 
         dtab_w = tile("dtab_w", [P, T], I32, "w_raw")
@@ -82,8 +80,8 @@ def tile_attend_tcpageratio_kernel(tc, dtab_words, dtab_scales, tab_words, tab_s
                                 rhs=tab_gw[:, slots].bitcast(FP8X4), rhs_scale=tab_gs[:, slots], start=True, stop=True)
             h0.append(tile("h0_%d" % s, [P, HALF], F32))
             nc.scalar.activation(h0[s][:], a[s][:], ACT.Tanh)
-        cpage = tile("cpage", [P, U], F32, "tab_w")
-        nc.vector.memset(cpage[:], 0.0)
+        dtab_gs = tile("dtab_gs", [P, J], U8)
+        nc.vector.tensor_copy(dtab_gs[:], dtab_s[:].indirect(offs_sb[:]))
         for s in range(2):
             entries = slice(s * HALF // 16, (s + 1) * HALF // 16)
             nc.vector.tensor_copy(pa[:].indirect(offs2_sb[:, entries]), h0[s][:])
@@ -99,24 +97,23 @@ def tile_attend_tcpageratio_kernel(tc, dtab_words, dtab_scales, tab_words, tab_s
         for s in range(2):
             slots = slice(s * HALF, (s + 1) * HALF)
             nc.scalar.activation(a_sq[:, slots], a[s][:], ACT.Square)
-            nc.scalar.activation(h_sq[:, slots], h0[s][:], ACT.Square)
+            nc.gpsimd.tensor_tensor(h_sq[:, slots], h0[s][:], h0[s][:], ALU.mult)
 
         a2 = tile("a2", [P, J], F32)
         curve = tile("curve", [P, J], F32)
         cvals = tile("cvals", [P, J], F32)
         xvals = tile("xvals", [P, J], F32)
-        for s in range(2):
-            slots = slice(s * HALF, (s + 1) * HALF)
-            nc.scalar.activation(a2[:, slots], a[s][:], ACT.Copy, scale=-2.0)
 
         gain_sb = tile("gain_sb", [P, 1], F32, "tab_s")
         og_sb = tile("og_sb", [P, 1], F32, "w_bf")
         nc.sync.dma_start(gain_sb[:], gain)
         nc.sync.dma_start(og_sb[:], og)
 
-        dtab_gs = tile("dtab_gs", [P, J], U8, "h0_0")
-        dtab_gw = tile("dtab_gw", [P, J], U32, "h0_1")
-        nc.vector.tensor_copy(dtab_gs[:], dtab_s[:].indirect(offs_sb[:]))
+        cpage = tile("cpage", [P, U], F32, "dtab_s")
+        xpage = tile("xpage", [P, U], F32, "h0_0")
+        nc.gpsimd.memset(cpage[:], 0.0)
+        nc.gpsimd.memset(xpage[:], 0.0)
+        dtab_gw = tile("dtab_gw", [P, J], U32)
         nc.vector.tensor_copy(dtab_gw[:], dtab_w[:].bitcast(U32).indirect(offs_sb[:]))
         ta = ps.tile([P, J], F32, name="ta")
         nc.tensor.matmul_mx(out=ta[:], lhsT=w_codes[:].bitcast(FP8X4), lhsT_scale=w_scales[:],
@@ -126,56 +123,66 @@ def tile_attend_tcpageratio_kernel(tc, dtab_words, dtab_scales, tab_words, tab_s
         nc.sync.dma_start(ground_sb[:], ground)
         nc.sync.dma_start(base_sb[:], base)
 
-        nc.scalar.activation(root[:], a_sq[:], ACT.Abs_reciprocal_sqrt, bias=1.0)
-        nc.scalar.activation(d1[:], root[:], ACT.Square)
+        for s in range(2):
+            slots = slice(s * HALF, (s + 1) * HALF)
+            nc.scalar.activation(root[:, slots], a_sq[:, slots], ACT.Abs_reciprocal_sqrt, bias=1.0)
+        for s in range(2):
+            slots = slice(s * HALF, (s + 1) * HALF)
+            nc.scalar.activation(d1[:, slots], root[:, slots], ACT.Square)
         nc.vector.tensor_copy(dpage[:].indirect(offs3_sb[:]), d1[:])
 
-        nc.scalar.activation(d2[:], d1[:], ACT.Square)
-        nc.gpsimd.tensor_tensor(curve[:], a2[:], d2[:], ALU.mult)
-        nc.scalar.activation(neg_gain[:], gain_sb[:], ACT.Copy, scale=-1.0)
-        nc.scalar.activation(slope[:], h_sq[:], ACT.Identity, scale=neg_gain[:], bias=gain_sb[:])
+        nc.gpsimd.tensor_scalar(neg_gain[:], gain_sb[:], -1.0, 0.0, ALU.mult, ALU.add)
+        nc.gpsimd.tensor_scalar(slope[:], h_sq[:], neg_gain[:], gain_sb[:], ALU.mult, ALU.add)
         nc.scalar.activation(ta_og[:], ta[:], ACT.Copy, scale=og_sb[:])
         nc.gpsimd.tensor_tensor(xvals[:], ta_og[:], slope[:], ALU.mult)
+        nc.scalar.activation(d2[:], d1[:], ACT.Square)
+        for s in range(2):
+            slots = slice(s * HALF, (s + 1) * HALF)
+            nc.scalar.activation(a2[:, slots], a[s][:], ACT.Copy, scale=-2.0)
+        nc.gpsimd.tensor_tensor(curve[:], a2[:], d2[:], ALU.mult)
         nc.vector.tensor_copy(xpage[:].indirect(offs2_sb[:]), xvals[:])
 
 
         nc.gpsimd.tensor_tensor(cvals[:], curve[:], ta_og[:], ALU.mult)
         nc.vector.tensor_copy(cpage[:].indirect(offs3_sb[:]), cvals[:])
 
-        def add_in_psum(name, x, y, tag, turned_tag):
-            turned = ps.tile([P, BANK], F32, name=name + "_turned", tag=turned_tag)
-            for b in range(BANK // P):
+        def add_in_psum(name, total, x, y, turned_tag):
+            width = x.shape[1]
+            turned = ps.tile([P, width], F32, name=name + "_turned", tag=turned_tag)
+            for b in range(width // P):
                 blk = slice(b * P, (b + 1) * P)
                 nc.tensor.matmul(turned[:, blk], lhsT=y[:, blk], rhs=ident[:], is_transpose=True, start=True, stop=False)
                 nc.tensor.matmul(turned[:, blk], lhsT=x[:, blk], rhs=ident[:], is_transpose=True, start=False, stop=True)
-            turned_sb = tile(name + "_turned_sb", [P, BANK], F32)
+            turned_sb = tile(name + "_turned_sb", [P, width], F32)
             nc.scalar.copy(turned_sb[:], turned[:])
-            total = ps.tile([P, BANK], F32, name=name, tag=tag)
-            for b in range(BANK // P):
+            for b in range(width // P):
                 blk = slice(b * P, (b + 1) * P)
                 nc.tensor.transpose(total[:, blk], turned_sb[:, blk], ident[:])
-            return total
 
         pa_g = tile("pa_g", [P, U], F32)
         t1 = []
         for half in range(U // BANK):
             cols = slice(half * BANK, (half + 1) * BANK)
             nc.scalar.activation(pa_g[:, cols], pa[:, cols], ACT.Copy, scale=gain_sb[:])
-            t1.append(add_in_psum("t1_%d" % half, pa_g[:, cols], ground_sb[:, cols], "t1_%d" % half, "turned%d" % half))
-        upage = tile("upage", [P, U], F32)
-        for half in range(U // BANK):
-            cols = slice(half * BANK, (half + 1) * BANK)
-            nc.gpsimd.tensor_tensor(upage[:, cols], xpage[:, cols], dpage[:, cols], ALU.mult)
+            t1.append(ps.tile([P, BANK], F32, name="t1_%d" % half))
+            add_in_psum("t1_%d" % half, t1[half][:], pa_g[:, cols], ground_sb[:, cols], "turned%d" % half)
+        upage = tile("upage", [P, U], F32, "curve")
+        v0 = ps.tile([P, BANK], F32, name="v0")
         v1 = tile("v1", [P, BANK], F32)
+        for q in range(2):
+            cols = slice(q * 256, (q + 1) * 256)
+            nc.gpsimd.tensor_tensor(upage[:, cols], xpage[:, cols], dpage[:, cols], ALU.mult)
+            add_in_psum("v0_%d" % q, v0[:, cols], upage[:, cols], base_sb[:, cols], "turned%d" % q)
+        nc.gpsimd.tensor_tensor(upage[:, BANK:U], xpage[:, BANK:U], dpage[:, BANK:U], ALU.mult)
         nc.gpsimd.tensor_tensor(v1[:], upage[:, BANK:U], base_sb[:, BANK:U], ALU.add)
-        v = [add_in_psum("v0", upage[:, 0:BANK], base_sb[:, 0:BANK], "v0", "turned0"), v1]
+        v = [v0, v1]
 
         prods = {}
-        for half in (1, 0):
+        for half in (0, 1):
             cols = slice(half * BANK, (half + 1) * BANK)
             prods[half] = tile("prod%d" % half, [P, BANK], F32)
             nc.vector.tensor_tensor(prods[half][:], cpage[:, cols], t1[half][:], ALU.mult)
-        for lo, hi in ((512, 1024), (0, 256), (256, 512)):
+        for lo, hi in ((0, 512), (512, 768), (768, 1024)):
             half, first = divmod(lo, BANK)
             cols = slice(first, first + hi - lo)
             res = tile("res%d" % lo, [P, hi - lo], F32)

from contextlib import ExitStack

import concourse.mybir as mybir
from concourse.masks import make_identity

F32 = mybir.dt.float32
BF16 = mybir.dt.bfloat16
U32 = mybir.dt.uint32
I32 = mybir.dt.int32
U16 = mybir.dt.uint16
U8 = mybir.dt.uint8
FP8X4 = mybir.dt.float8_e4m3fn_x4
ACT = mybir.ActivationFunctionType
ALU = mybir.AluOpType

P = 128
K, R, T, J, U = 512, 128, 2048, 512, 1024
BANK = 512
FLOPS = 2 * 2 * K * R * J


def tile_attend_tcpageratio_kernel(tc, dtab_words, dtab_scales, tab_words, tab_scales, w1, gain, ground, og, base, offs, offs2, offs3, out):
    nc = tc.nc
    with ExitStack() as ctx:
        sb = ctx.enter_context(tc.tile_pool(name="sb", bufs=1))
        ps = ctx.enter_context(tc.psum_pool(name="ps", bufs=1))

        def tile(name, shape, dtype, tag=None):
            return sb.tile(shape, dtype, name=name, tag=tag or name, align_bytes=64)

        offs_sb = tile("offs_sb", [P, J // 16], U16)
        offs2_sb = tile("offs2_sb", [P, J // 16], U16)
        offs3_sb = tile("offs3_sb", [P, J // 16], U16)
        w_raw = tile("w_raw", [P, 4, R], F32)
        tab_w = tile("tab_w", [P, T], I32)
        tab_s = tile("tab_s", [P, T], U8)
        dtab_s = tile("dtab_s", [P, T], U8)

        nc.gpsimd.memset(tab_s[:].bitcast(I32), 0)
        nc.gpsimd.memset(dtab_s[:].bitcast(I32), 0)
        nc.sync.dma_start(offs_sb[:], offs)
        nc.sync.dma_start(offs2_sb[:], offs2)
        nc.sync.dma_start(w_raw[:], w1.rearrange("(p t) r -> p t r", t=4))
        for i in range(4):
            nc.sync.dma_start(tab_s[i:P:32, :].bitcast(I32), tab_scales[0, i:16:4, :].bitcast(I32))
        nc.sync.dma_start(tab_w[:], tab_words[0].rearrange("p c t -> p (c t)").bitcast(I32))

        w_bf = tile("w_bf", [P, R, 4], BF16)
        w_codes = tile("w_codes", [P, R], U32)
        w_scales = tile("w_scales", [P, R], U8)
        nc.vector.tensor_copy(w_bf[:], w_raw[:].rearrange("p t r -> p r t"))
        nc.vector.quantize_mx(out=w_codes[:].bitcast(FP8X4), scales=w_scales[:], in_=w_bf[:].rearrange("p r t -> p (r t)"))

        pa = tile("pa", [P, U], F32)
        dpage = tile("dpage", [P, U], F32)
        ident = tile("ident", [P, P], F32)
        nc.vector.memset(pa[:], 0.0)
        nc.vector.memset(dpage[:], 1.0)
        make_identity(nc, ident[:])
        for i in range(4):
            nc.sync.dma_start(dtab_s[i:P:32, :].bitcast(I32), dtab_scales[0, i:16:4, :].bitcast(I32))
        nc.sync.dma_start(offs3_sb[:], offs3)


        dtab_w = tile("dtab_w", [P, T], I32, "w_raw")
        nc.sync.dma_start(dtab_w[:], dtab_words[0].rearrange("p c t -> p (c t)").bitcast(I32))

        HALF = J // 2
        tab_gs = tile("tab_gs", [P, J], U8)
        tab_gw = tile("tab_gw", [P, J], U32)
        nc.vector.tensor_copy(tab_gs[:], tab_s[:].indirect(offs_sb[:]))
        a = []
        h0 = []
        for s in range(2):
            slots = slice(s * HALF, (s + 1) * HALF)
            entries = slice(s * HALF // 16, (s + 1) * HALF // 16)
            nc.vector.tensor_copy(tab_gw[:, slots], tab_w[:].bitcast(U32).indirect(offs_sb[:, entries]))
            a.append(ps.tile([P, HALF], F32, name="a%d" % s))
            nc.tensor.matmul_mx(out=a[s][:], lhsT=w_codes[:].bitcast(FP8X4), lhsT_scale=w_scales[:],
                                rhs=tab_gw[:, slots].bitcast(FP8X4), rhs_scale=tab_gs[:, slots], start=True, stop=True)
            h0.append(tile("h0_%d" % s, [P, HALF], F32))
            nc.scalar.activation(h0[s][:], a[s][:], ACT.Tanh)
        dtab_gs = tile("dtab_gs", [P, J], U8)
        nc.vector.tensor_copy(dtab_gs[:], dtab_s[:].indirect(offs_sb[:]))
        for s in range(2):
            entries = slice(s * HALF // 16, (s + 1) * HALF // 16)
            nc.vector.tensor_copy(pa[:].indirect(offs2_sb[:, entries]), h0[s][:])

        a_sq = tile("a_sq", [P, J], F32)
        root = tile("root", [P, J], F32)
        d1 = tile("d1", [P, J], F32)
        d2 = tile("d2", [P, J], F32)
        h_sq = tile("h_sq", [P, J], F32)
        slope = tile("slope", [P, J], F32)
        ta_og = tile("ta_og", [P, J], F32)
        neg_gain = tile("neg_gain", [P, 1], F32)
        for s in range(2):
            slots = slice(s * HALF, (s + 1) * HALF)
            nc.scalar.activation(a_sq[:, slots], a[s][:], ACT.Square)
            nc.gpsimd.tensor_tensor(h_sq[:, slots], h0[s][:], h0[s][:], ALU.mult)

        a2 = tile("a2", [P, J], F32)
        curve = tile("curve", [P, J], F32)
        cvals = tile("cvals", [P, J], F32)
        xvals = tile("xvals", [P, J], F32)

        gain_sb = tile("gain_sb", [P, 1], F32, "tab_s")
        og_sb = tile("og_sb", [P, 1], F32, "w_bf")
        nc.sync.dma_start(gain_sb[:], gain)
        nc.sync.dma_start(og_sb[:], og)

        cpage = tile("cpage", [P, U], F32, "dtab_s")
        xpage = tile("xpage", [P, U], F32, "h0_0")
        nc.gpsimd.memset(cpage[:], 0.0)
        nc.gpsimd.memset(xpage[:], 0.0)
        dtab_gw = tile("dtab_gw", [P, J], U32)
        nc.vector.tensor_copy(dtab_gw[:], dtab_w[:].bitcast(U32).indirect(offs_sb[:]))
        ta = ps.tile([P, J], F32, name="ta")
        nc.tensor.matmul_mx(out=ta[:], lhsT=w_codes[:].bitcast(FP8X4), lhsT_scale=w_scales[:],
                            rhs=dtab_gw[:].bitcast(FP8X4), rhs_scale=dtab_gs[:], start=True, stop=True)
        ground_sb = tile("ground_sb", [P, U], F32, "tab_gw")
        base_sb = tile("base_sb", [P, U], F32, "tab_gs")
        nc.sync.dma_start(ground_sb[:], ground)
        nc.sync.dma_start(base_sb[:], base)

        for s in range(2):
            slots = slice(s * HALF, (s + 1) * HALF)
            nc.scalar.activation(root[:, slots], a_sq[:, slots], ACT.Abs_reciprocal_sqrt, bias=1.0)
        for s in range(2):
            slots = slice(s * HALF, (s + 1) * HALF)
            nc.scalar.activation(d1[:, slots], root[:, slots], ACT.Square)
        nc.vector.tensor_copy(dpage[:].indirect(offs3_sb[:]), d1[:])

        nc.gpsimd.tensor_scalar(neg_gain[:], gain_sb[:], -1.0, 0.0, ALU.mult, ALU.add)
        nc.gpsimd.tensor_scalar(slope[:], h_sq[:], neg_gain[:], gain_sb[:], ALU.mult, ALU.add)
        nc.scalar.activation(ta_og[:], ta[:], ACT.Copy, scale=og_sb[:])
        nc.gpsimd.tensor_tensor(xvals[:], ta_og[:], slope[:], ALU.mult)
        nc.scalar.activation(d2[:], d1[:], ACT.Square)
        for s in range(2):
            slots = slice(s * HALF, (s + 1) * HALF)
            nc.scalar.activation(a2[:, slots], a[s][:], ACT.Copy, scale=-2.0)
        nc.gpsimd.tensor_tensor(curve[:], a2[:], d2[:], ALU.mult)
        nc.vector.tensor_copy(xpage[:].indirect(offs2_sb[:]), xvals[:])


        nc.gpsimd.tensor_tensor(cvals[:], curve[:], ta_og[:], ALU.mult)
        nc.vector.tensor_copy(cpage[:].indirect(offs3_sb[:]), cvals[:])

        def add_in_psum(name, total, x, y, turned_tag):
            width = x.shape[1]
            turned = ps.tile([P, width], F32, name=name + "_turned", tag=turned_tag)
            for b in range(width // P):
                blk = slice(b * P, (b + 1) * P)
                nc.tensor.matmul(turned[:, blk], lhsT=y[:, blk], rhs=ident[:], is_transpose=True, start=True, stop=False)
                nc.tensor.matmul(turned[:, blk], lhsT=x[:, blk], rhs=ident[:], is_transpose=True, start=False, stop=True)
            turned_sb = tile(name + "_turned_sb", [P, width], F32)
            nc.scalar.copy(turned_sb[:], turned[:])
            for b in range(width // P):
                blk = slice(b * P, (b + 1) * P)
                nc.tensor.transpose(total[:, blk], turned_sb[:, blk], ident[:])

        pa_g = tile("pa_g", [P, U], F32)
        t1 = []
        for half in range(U // BANK):
            cols = slice(half * BANK, (half + 1) * BANK)
            nc.scalar.activation(pa_g[:, cols], pa[:, cols], ACT.Copy, scale=gain_sb[:])
            t1.append(ps.tile([P, BANK], F32, name="t1_%d" % half))
            add_in_psum("t1_%d" % half, t1[half][:], pa_g[:, cols], ground_sb[:, cols], "turned%d" % half)
        upage = tile("upage", [P, U], F32, "curve")
        v0 = ps.tile([P, BANK], F32, name="v0")
        v1 = tile("v1", [P, BANK], F32)
        for q in range(2):
            cols = slice(q * 256, (q + 1) * 256)
            nc.gpsimd.tensor_tensor(upage[:, cols], xpage[:, cols], dpage[:, cols], ALU.mult)
            add_in_psum("v0_%d" % q, v0[:, cols], upage[:, cols], base_sb[:, cols], "turned%d" % q)
        nc.gpsimd.tensor_tensor(upage[:, BANK:U], xpage[:, BANK:U], dpage[:, BANK:U], ALU.mult)
        nc.gpsimd.tensor_tensor(v1[:], upage[:, BANK:U], base_sb[:, BANK:U], ALU.add)
        v = [v0, v1]

        prods = {}
        for half in (0, 1):
            cols = slice(half * BANK, (half + 1) * BANK)
            prods[half] = tile("prod%d" % half, [P, BANK], F32)
            nc.vector.tensor_tensor(prods[half][:], cpage[:, cols], t1[half][:], ALU.mult)
        for lo, hi in ((0, 512), (512, 768), (768, 1024)):
            half, first = divmod(lo, BANK)
            cols = slice(first, first + hi - lo)
            res = tile("res%d" % lo, [P, hi - lo], F32)
            nc.vector.tensor_tensor(res[:], prods[half][:, cols], v[half][:, cols], ALU.add)
            nc.sync.dma_start(out[:, lo:hi], res[:])
